import numpy as np, ml_dtypes
CORES = [19,27,51,107,147,155,179,235,275,283,307,363,403,411,435,491]
N = 16
TK, NT = 512, 8
def setup_inputs(rng):
    x = rng.standard_normal((NT, 128, TK), dtype=np.float32).astype(ml_dtypes.bfloat16)
    return {"x": np.broadcast_to(x, (2, NT, 128, TK)).reshape(N, 128, TK).copy(), "w": rng.standard_normal((N, 128, NT * 128), dtype=np.float32).astype(ml_dtypes.bfloat16)}
def setup_inputs_big(rng):
    d = setup_inputs(rng)
    for k in ("x", "w"): d[k] = (d[k].astype(np.float32) * 1024.0).astype(d[k].dtype)
    return d
def setup_inputs_small(rng):
    d = setup_inputs(rng)
    for k in ("x", "w"): d[k] = (d[k].astype(np.float32) * (1 / 1024.0)).astype(d[k].dtype)
    return d
def setup_inputs_apart(rng):
    d = setup_inputs(rng)
    f = (10.0 ** rng.permutation(np.linspace(-1.5, 1.5, N))).astype(np.float32).reshape(N, 1, 1)
    for k in ("x", "w"): d[k] = (d[k].astype(np.float32) * f).astype(d[k].dtype)
    return d
def tie_inputs(x):
    x = dict(x)
    x["x"] = np.concatenate([x["x"][:NT], x["x"][:NT]])
    return x
def reference(x, w):
    X, W = x.astype(np.float64), w.astype(np.float64)
    y = np.stack([sum(W[r][:, 128 * j:128 * j + 128].T @ X[j if r < NT else j + NT] for j in range(NT)) for r in range(N)])
    return {"y": y.astype(ml_dtypes.bfloat16 if x.dtype != np.float64 else np.float64)}

@@ -1,0 +1,95 @@
+from concourse.bass import DstId, RemoteDMATransfer
+
+P, TK, TM, NT = 128, 512, 128, 8
+HALF = TK // 2
+
+STEPS = ((1, 2), (3, 6), (5, 7), (4,))
+
+SCRATCH = {
+    "xg": ("sbuf", [P, NT * TK], "bfloat16"),
+    "ws": ("sbuf", [P, NT * TM], "bfloat16"),
+    "ys": ("sbuf", [P, TK], "bfloat16"),
+    "acc0": ("psum", [P, TK], "float32"),
+    "acc1": ("psum", [P, TK], "float32"),
+}
+SEMAPHORES = ["ldx", "ldw", "mm0", "mm1", "cp", "st", "sent"] + ["xa%d" % j for j in range(NT)]
+
+
+def _engines(mask):
+    return [e for e in range(mask.bit_length()) if (mask >> e) & 1]
+
+
+def _bits(engines):
+    m = 0
+    for e in engines:
+        m |= 1 << e
+    return m
+
+
+def _ring(core, T, topo):
+    rack = topo.rack(topo.host(core))
+    return {T.rank_of(c) % NT: c for c in T.cores if topo.rack(topo.host(c)) == rack}
+
+
+def _calls(src, ring, T, topo):
+    me = T.rank_of(src) % NT
+    mask = -1
+    for call in STEPS:
+        for k in call:
+            mask &= topo.mask(src, ring[(me + k) % NT])
+    eng = _engines(mask)
+    out = []
+    for call in STEPS:
+        n = len(eng) // len(call)
+        out.append([(k, ring[(me + k) % NT], eng[i * n:(i + 1) * n]) for i, k in enumerate(call)])
+    return out
+
+
+def rank_program(g, core, T, topo):
+    if T.rank_of(core) is None:
+        return
+    S = T.sem
+    ring = _ring(core, T, topo)
+    me = T.rank_of(core) % NT
+
+    def slot(j, lo=0, hi=TK):
+        return T.xg[:, TK * j + lo:TK * j + hi]
+
+    g.sync.dma_start(slot(me), T.x[:]).then_inc(S.ldx, 16)
+    g.scalar.dma_start(T.ws[:], T.w[:]).then_inc(S.ldw, 16)
+
+    g.wait_ge(S.ldx, 16)
+    left = 0
+    for call in _calls(core, ring, T, topo):
+        transfers = []
+        for k, dst, eng in call:
+            rid, pid = topo.addr(dst, core)
+            transfers.append(RemoteDMATransfer(dst_ids=[DstId(rid=rid, pnc=pid)], dma_engine_mask=_bits(eng),
+                                               remote_sem=S["xa%d" % me], src=slot(me), dst=slot(me)))
+            left += len(eng)
+        g.remote_dma_fused(transfers, local_sem=S.sent)
+
+    te = g.tensor
+    te.wait_ge(S.ldw, 16)
+    te.wait_ge(S.ldx, 16)
+    order = [0] + [k for call in STEPS for k in call]
+    acc = (T.acc0, T.acc1)
+    for n, k in enumerate(order):
+        j = (me - k) % NT
+        if k:
+            count = [len(eng) for call in _calls(ring[j], ring, T, topo) for kk, dst, eng in call if kk == k][0]
+            te.wait_ge(S["xa%d" % j], count)
+        for h in range(2):
+            mm = te.matmul(acc[h][:, 0:HALF], T.ws[:, TM * j:TM * (j + 1)], slot(j, HALF * h, HALF * (h + 1)),
+                           n == 0, n == len(order) - 1)
+            if n == len(order) - 1:
+                mm.then_inc(S["mm%d" % h], 1)
+
+    ve = g.vector
+    for h in range(2):
+        ve.wait_ge(S["mm%d" % h], 1)
+        ve.tensor_copy(T.ys[:, HALF * h:HALF * (h + 1)], acc[h][:, 0:HALF]).then_inc(S.cp, 1)
+    g.sync.wait_ge(S.cp, 2)
+    g.sync.dma_start(T.y[:], T.ys[:]).then_inc(S.st, 16)
+    g.sync.wait_ge(S.st, 16)
+    g.wait_ge(S.sent, left)

@@ -3,7 +3,9 @@ from concourse.bass import DstId, RemoteDMATransfer
 P, TK, TM, NT = 128, 512, 128, 8
 HALF = TK // 2
 
-STEPS = ((1, 2), (3, 6), (5, 7), (4,))
+DIRECT = ((1, 2), (3, 6), (4,))
+HELPED = (((5, 7),),)
+ORDER = (1, 2, 3, 6, 4, 5, 7)
 
 SCRATCH = {
     "xg": ("sbuf", [P, NT * TK], "bfloat16"),
@@ -26,58 +28,94 @@ def _bits(engines):
     return m
 
 
-def _ring(core, T, topo):
-    rack = topo.rack(topo.host(core))
-    return {T.rank_of(c) % NT: c for c in T.cores if topo.rack(topo.host(c)) == rack}
+def _plan(rc, T, topo):
+    rack = topo.rack(topo.host(rc))
+    ring = {T.rank_of(c) % NT: c for c in T.cores if topo.rack(topo.host(c)) == rack}
+    me = T.rank_of(rc) % NT
 
+    def calls(src, steps):
+        mask = -1
+        for call in steps:
+            for k in call:
+                mask &= topo.mask(src, ring[(me + k) % NT])
+        eng = _engines(mask)
+        out = []
+        for call in steps:
+            n = len(eng) // len(call)
+            out.append([(k, ring[(me + k) % NT], eng[i * n:(i + 1) * n]) for i, k in enumerate(call)])
+        return out, mask
 
-def _calls(src, ring, T, topo):
-    me = T.rank_of(src) % NT
-    mask = -1
-    for call in STEPS:
-        for k in call:
-            mask &= topo.mask(src, ring[(me + k) % NT])
-    eng = _engines(mask)
-    out = []
-    for call in STEPS:
-        n = len(eng) // len(call)
-        out.append([(k, ring[(me + k) % NT], eng[i * n:(i + 1) * n]) for i, k in enumerate(call)])
-    return out
+    w = topo.CORES_PER_CHIP
+    chipmates = [c for c in range(max(rc - w, 0), rc + w)
+                 if c != rc and topo.host(c) == topo.host(rc) and topo.chip(c) == topo.chip(rc) and topo.die(c) != topo.die(rc)]
+    chipmates.sort(key=lambda c: sum(1 for d in ring.values() if topo.may_write(c, d)))
+    helpers, by_sender = [], {}
+    by_sender[rc], off = calls(rc, DIRECT)
+    for steps in HELPED:
+        h = [c for c in chipmates if c not in helpers
+             and all(topo.may_write(c, ring[(me + k) % NT]) for call in steps for k in call)][0]
+        helpers.append(h)
+        by_sender[h] = calls(h, steps)[0]
+    hand = []
+    if helpers:
+        free = -1
+        for h in helpers:
+            free &= topo.mask(rc, h)
+        free = _engines(free & ~off)
+        n = 1
+        while n * 2 * len(helpers) <= len(free):
+            n *= 2
+        hand = [free[i * n:(i + 1) * n] for i in range(len(helpers))]
+    return me, ring, helpers, by_sender, hand
 
 
 def rank_program(g, core, T, topo):
-    if T.rank_of(core) is None:
-        return
     S = T.sem
-    ring = _ring(core, T, topo)
-    me = T.rank_of(core) % NT
 
     def slot(j, lo=0, hi=TK):
         return T.xg[:, TK * j + lo:TK * j + hi]
 
+    def send(me, calls):
+        left = 0
+        for call in calls:
+            transfers = []
+            for k, dst, eng in call:
+                rid, pid = topo.addr(dst, core)
+                transfers.append(RemoteDMATransfer(dst_ids=[DstId(rid=rid, pnc=pid)], dma_engine_mask=_bits(eng),
+                                                   remote_sem=S["xa%d" % me], src=slot(me), dst=slot(me)))
+                left += len(eng)
+            g.remote_dma_fused(transfers, local_sem=S.sent)
+        return left
+
+    if T.rank_of(core) is None:
+        owner = [c for c in T.cores if topo.host(c) == topo.host(core) and topo.chip(c) == topo.chip(core)]
+        if not owner:
+            return
+        me, ring, helpers, by_sender, hand = _plan(owner[0], T, topo)
+        if core not in helpers:
+            return
+        g.wait_ge(S["xa%d" % me], len(hand[helpers.index(core)]))
+        g.wait_ge(S.sent, send(me, by_sender[core]))
+        return
+
+    me, ring, helpers, by_sender, hand = _plan(core, T, topo)
     g.sync.dma_start(slot(me), T.x[:]).then_inc(S.ldx, 16)
     g.scalar.dma_start(T.ws[:], T.w[:]).then_inc(S.ldw, 16)
 
     g.wait_ge(S.ldx, 16)
-    left = 0
-    for call in _calls(core, ring, T, topo):
-        transfers = []
-        for k, dst, eng in call:
-            rid, pid = topo.addr(dst, core)
-            transfers.append(RemoteDMATransfer(dst_ids=[DstId(rid=rid, pnc=pid)], dma_engine_mask=_bits(eng),
-                                               remote_sem=S["xa%d" % me], src=slot(me), dst=slot(me)))
-            left += len(eng)
-        g.remote_dma_fused(transfers, local_sem=S.sent)
+    left = send(me, [[(0, h, e) for h, e in zip(helpers, hand)]]) if helpers else 0
+    left += send(me, by_sender[core])
 
     te = g.tensor
     te.wait_ge(S.ldw, 16)
     te.wait_ge(S.ldx, 16)
-    order = [0] + [k for call in STEPS for k in call]
+    order = (0,) + ORDER
     acc = (T.acc0, T.acc1)
     for n, k in enumerate(order):
         j = (me - k) % NT
         if k:
-            count = [len(eng) for call in _calls(ring[j], ring, T, topo) for kk, dst, eng in call if kk == k][0]
+            theirs = _plan(ring[j], T, topo)[3]
+            count = [len(eng) for calls in theirs.values() for call in calls for kk, dst, eng in call if kk == k][0]
             te.wait_ge(S["xa%d" % j], count)
         for h in range(2):
             mm = te.matmul(acc[h][:, 0:HALF], T.ws[:, TM * j:TM * (j + 1)], slot(j, HALF * h, HALF * (h + 1)),

@@ -2,10 +2,11 @@ from concourse.bass import DstId, RemoteDMATransfer
 
 P, TK, TM, NT = 128, 512, 128, 8
 HALF = TK // 2
+W, L, R = None, 0, 1
 
-DIRECT = ((1, 2), (3, 6), (4,))
-HELPED = (((5, 7),),)
-ORDER = (1, 2, 3, 6, 4, 5, 7)
+DIRECT = (((1, W), (2, W)), ((3, W),), ((6, W),), ((7, R),))
+HELPED = ((((5, W),), ((7, L),)), (((4, W),),))
+ORDER = ((1, W), (2, W), (3, W), (5, W), (6, W), (7, L), (4, W), (7, R))
 
 SCRATCH = {
     "xg": ("sbuf", [P, NT * TK], "bfloat16"),
@@ -14,7 +15,8 @@ SCRATCH = {
     "acc0": ("psum", [P, TK], "float32"),
     "acc1": ("psum", [P, TK], "float32"),
 }
-SEMAPHORES = ["ldx", "ldw", "mm0", "mm1", "cp", "st", "sent"] + ["xa%d" % j for j in range(NT)]
+SEMAPHORES = (["ldx", "ldw", "mm0", "mm1", "cp", "st", "sent"] + ["xa%d" % j for j in range(NT)]
+              + ["xb%d" % j for j in range(NT)])
 
 
 def _engines(mask):
@@ -36,13 +38,13 @@ def _plan(rc, T, topo):
     def calls(src, steps):
         mask = -1
         for call in steps:
-            for k in call:
+            for k, part in call:
                 mask &= topo.mask(src, ring[(me + k) % NT])
         eng = _engines(mask)
         out = []
         for call in steps:
             n = len(eng) // len(call)
-            out.append([(k, ring[(me + k) % NT], eng[i * n:(i + 1) * n]) for i, k in enumerate(call)])
+            out.append([(k, part, ring[(me + k) % NT], eng[i * n:(i + 1) * n]) for i, (k, part) in enumerate(call)])
         return out, mask
 
     w = topo.CORES_PER_CHIP
@@ -53,36 +55,34 @@ def _plan(rc, T, topo):
     by_sender[rc], off = calls(rc, DIRECT)
     for steps in HELPED:
         h = [c for c in chipmates if c not in helpers
-             and all(topo.may_write(c, ring[(me + k) % NT]) for call in steps for k in call)][0]
+             and all(topo.may_write(c, ring[(me + k) % NT]) for call in steps for k, part in call)][0]
         helpers.append(h)
         by_sender[h] = calls(h, steps)[0]
-    hand = []
-    if helpers:
-        free = -1
-        for h in helpers:
-            free &= topo.mask(rc, h)
-        free = _engines(free & ~off)
-        n = 1
-        while n * 2 * len(helpers) <= len(free):
-            n *= 2
-        hand = [free[i * n:(i + 1) * n] for i in range(len(helpers))]
+    free = -1
+    for h in helpers:
+        free &= topo.mask(rc, h)
+    hand = [_engines(free & ~off)] * len(helpers)
     return me, ring, helpers, by_sender, hand
 
 
 def rank_program(g, core, T, topo):
     S = T.sem
 
-    def slot(j, lo=0, hi=TK):
+    def slot(j, part=W):
+        lo, hi = (0, TK) if part is W else (HALF * part, HALF * (part + 1))
         return T.xg[:, TK * j + lo:TK * j + hi]
+
+    def landed(j, part):
+        return S[("xb%d" if part == R else "xa%d") % j]
 
     def send(me, calls):
         left = 0
         for call in calls:
             transfers = []
-            for k, dst, eng in call:
+            for k, part, dst, eng in call:
                 rid, pid = topo.addr(dst, core)
                 transfers.append(RemoteDMATransfer(dst_ids=[DstId(rid=rid, pnc=pid)], dma_engine_mask=_bits(eng),
-                                                   remote_sem=S["xa%d" % me], src=slot(me), dst=slot(me)))
+                                                   remote_sem=landed(me, part), src=slot(me, part), dst=slot(me, part)))
                 left += len(eng)
             g.remote_dma_fused(transfers, local_sem=S.sent)
         return left
@@ -94,37 +94,40 @@ def rank_program(g, core, T, topo):
         me, ring, helpers, by_sender, hand = _plan(owner[0], T, topo)
         if core not in helpers:
             return
-        g.wait_ge(S["xa%d" % me], len(hand[helpers.index(core)]))
+        g.wait_ge(landed(me, W), len(hand[helpers.index(core)]))
         g.wait_ge(S.sent, send(me, by_sender[core]))
         return
 
     me, ring, helpers, by_sender, hand = _plan(core, T, topo)
     g.sync.dma_start(slot(me), T.x[:]).then_inc(S.ldx, 16)
-    g.scalar.dma_start(T.ws[:], T.w[:]).then_inc(S.ldw, 16)
+    g.sync.dma_start(T.ws[:], T.w[:]).then_inc(S.ldw, 16)
 
     g.wait_ge(S.ldx, 16)
-    left = send(me, [[(0, h, e) for h, e in zip(helpers, hand)]]) if helpers else 0
+    left = send(me, [[(0, W, h, e)] for h, e in zip(helpers, hand)])
     left += send(me, by_sender[core])
 
     te = g.tensor
     te.wait_ge(S.ldw, 16)
     te.wait_ge(S.ldx, 16)
-    order = (0,) + ORDER
     acc = (T.acc0, T.acc1)
-    for n, k in enumerate(order):
+    work = []
+    for k, part in ((0, W),) + ORDER:
+        for n, h in enumerate((L, R) if part is W else (part,)):
+            work.append((k, part if (k and n == 0) else -1, h))
+    last = {h: max(n for n, item in enumerate(work) if item[2] == h) for h in (L, R)}
+    for n, (k, part, h) in enumerate(work):
         j = (me - k) % NT
-        if k:
+        if part != -1:
             theirs = _plan(ring[j], T, topo)[3]
-            count = [len(eng) for calls in theirs.values() for call in calls for kk, dst, eng in call if kk == k][0]
-            te.wait_ge(S["xa%d" % j], count)
-        for h in range(2):
-            mm = te.matmul(acc[h][:, 0:HALF], T.ws[:, TM * j:TM * (j + 1)], slot(j, HALF * h, HALF * (h + 1)),
-                           n == 0, n == len(order) - 1)
-            if n == len(order) - 1:
-                mm.then_inc(S["mm%d" % h], 1)
+            count = [len(eng) for calls in theirs.values() for call in calls for kk, pp, dst, eng in call
+                     if (kk, pp) == (k, part)][0]
+            te.wait_ge(landed(j, part), count)
+        mm = te.matmul(acc[h][:, 0:HALF], T.ws[:, TM * j:TM * (j + 1)], slot(j, h), k == 0, n == last[h])
+        if n == last[h]:
+            mm.then_inc(S["mm%d" % h], 1)
 
     ve = g.vector
-    for h in range(2):
+    for h in (L, R):
         ve.wait_ge(S["mm%d" % h], 1)
         ve.tensor_copy(T.ys[:, HALF * h:HALF * (h + 1)], acc[h][:, 0:HALF]).then_inc(S.cp, 1)
     g.sync.wait_ge(S.cp, 2)

from concourse.bass import DstId, RemoteDMATransfer

P, TK, TM, NT = 128, 512, 128, 8
HALF = TK // 2
W, L, R = None, 0, 1

DIRECT = (((1, W), (2, W)), ((3, W),), ((6, W),), ((7, R),))
HELPED = ((((5, W),), ((7, L),)), (((4, W),),))
ORDER = ((1, W), (2, W), (3, W), (5, W), (6, W), (7, L), (4, W), (7, R))

SCRATCH = {
    "xg": ("sbuf", [P, NT * TK], "bfloat16"),
    "ws": ("sbuf", [P, NT * TM], "bfloat16"),
    "ys": ("sbuf", [P, TK], "bfloat16"),
    "acc0": ("psum", [P, TK], "float32"),
    "acc1": ("psum", [P, TK], "float32"),
}
SEMAPHORES = (["ldx", "ldw", "mm0", "mm1", "cp", "st", "sent"] + ["xa%d" % j for j in range(NT)]
              + ["xb%d" % j for j in range(NT)])


def _engines(mask):
    return [e for e in range(mask.bit_length()) if (mask >> e) & 1]


def _bits(engines):
    m = 0
    for e in engines:
        m |= 1 << e
    return m


def _plan(rc, T, topo):
    rack = topo.rack(topo.host(rc))
    ring = {T.rank_of(c) % NT: c for c in T.cores if topo.rack(topo.host(c)) == rack}
    me = T.rank_of(rc) % NT

    def calls(src, steps):
        mask = -1
        for call in steps:
            for k, part in call:
                mask &= topo.mask(src, ring[(me + k) % NT])
        eng = _engines(mask)
        out = []
        for call in steps:
            n = len(eng) // len(call)
            out.append([(k, part, ring[(me + k) % NT], eng[i * n:(i + 1) * n]) for i, (k, part) in enumerate(call)])
        return out, mask

    w = topo.CORES_PER_CHIP
    chipmates = [c for c in range(max(rc - w, 0), rc + w)
                 if c != rc and topo.host(c) == topo.host(rc) and topo.chip(c) == topo.chip(rc) and topo.die(c) != topo.die(rc)]
    chipmates.sort(key=lambda c: sum(1 for d in ring.values() if topo.may_write(c, d)))
    helpers, by_sender = [], {}
    by_sender[rc], off = calls(rc, DIRECT)
    for steps in HELPED:
        h = [c for c in chipmates if c not in helpers
             and all(topo.may_write(c, ring[(me + k) % NT]) for call in steps for k, part in call)][0]
        helpers.append(h)
        by_sender[h] = calls(h, steps)[0]
    free = -1
    for h in helpers:
        free &= topo.mask(rc, h)
    hand = [_engines(free & ~off)] * len(helpers)
    return me, ring, helpers, by_sender, hand


def rank_program(g, core, T, topo):
    S = T.sem

    def slot(j, part=W):
        lo, hi = (0, TK) if part is W else (HALF * part, HALF * (part + 1))
        return T.xg[:, TK * j + lo:TK * j + hi]

    def landed(j, part):
        return S[("xb%d" if part == R else "xa%d") % j]

    def send(me, calls):
        left = 0
        for call in calls:
            transfers = []
            for k, part, dst, eng in call:
                rid, pid = topo.addr(dst, core)
                transfers.append(RemoteDMATransfer(dst_ids=[DstId(rid=rid, pnc=pid)], dma_engine_mask=_bits(eng),
                                                   remote_sem=landed(me, part), src=slot(me, part), dst=slot(me, part)))
                left += len(eng)
            g.remote_dma_fused(transfers, local_sem=S.sent)
        return left

    if T.rank_of(core) is None:
        owner = [c for c in T.cores if topo.host(c) == topo.host(core) and topo.chip(c) == topo.chip(core)]
        if not owner:
            return
        me, ring, helpers, by_sender, hand = _plan(owner[0], T, topo)
        if core not in helpers:
            return
        g.wait_ge(landed(me, W), len(hand[helpers.index(core)]))
        g.wait_ge(S.sent, send(me, by_sender[core]))
        return

    me, ring, helpers, by_sender, hand = _plan(core, T, topo)
    g.sync.dma_start(slot(me), T.x[:]).then_inc(S.ldx, 16)
    g.sync.dma_start(T.ws[:], T.w[:]).then_inc(S.ldw, 16)

    g.wait_ge(S.ldx, 16)
    left = send(me, [[(0, W, h, e)] for h, e in zip(helpers, hand)])
    left += send(me, by_sender[core])

    te = g.tensor
    te.wait_ge(S.ldw, 16)
    te.wait_ge(S.ldx, 16)
    acc = (T.acc0, T.acc1)
    work = []
    for k, part in ((0, W),) + ORDER:
        for n, h in enumerate((L, R) if part is W else (part,)):
            work.append((k, part if (k and n == 0) else -1, h))
    last = {h: max(n for n, item in enumerate(work) if item[2] == h) for h in (L, R)}
    for n, (k, part, h) in enumerate(work):
        j = (me - k) % NT
        if part != -1:
            theirs = _plan(ring[j], T, topo)[3]
            count = [len(eng) for calls in theirs.values() for call in calls for kk, pp, dst, eng in call
                     if (kk, pp) == (k, part)][0]
            te.wait_ge(landed(j, part), count)
        mm = te.matmul(acc[h][:, 0:HALF], T.ws[:, TM * j:TM * (j + 1)], slot(j, h), k == 0, n == last[h])
        if n == last[h]:
            mm.then_inc(S["mm%d" % h], 1)

    ve = g.vector
    for h in (L, R):
        ve.wait_ge(S["mm%d" % h], 1)
        ve.tensor_copy(T.ys[:, HALF * h:HALF * (h + 1)], acc[h][:, 0:HALF]).then_inc(S.cp, 1)
    g.sync.wait_ge(S.cp, 2)
    g.sync.dma_start(T.y[:], T.ys[:]).then_inc(S.st, 16)
    g.sync.wait_ge(S.st, 16)
    g.wait_ge(S.sent, left)
